import numpy as np
import ml_dtypes

BF16 = ml_dtypes.bfloat16


def bf(x):
    return np.asarray(x, np.float32).astype(BF16)


def f32(x):
    return np.asarray(x, np.float32)


def f64(x):
    return np.asarray(x).astype(np.float64)


def striped(idx):
    return np.tile(idx.reshape(-1, 16).T, (8, 1))


S, K, M, N, B, Q = 256, 512, 128, 256, 2, 128


def setup_inputs():
    return {"base": bf(np.random.standard_normal((B, M, S))), "x": bf(np.random.standard_normal((K, N))), "w": bf(np.random.standard_normal((K, M)) / np.sqrt(K)), "c": f32(0.2 + 0.8 * np.random.random_sample((1, S))), "offs": striped(np.random.permutation(S))}


def reference(base, x, w, c, offs):
    idx = offs[:16].T.reshape(-1)
    z = f64(base).copy()
    for i in range(B):
        z[i][:, idx[i * Q : (i + 1) * Q]] += f64(w).T @ f64(x)[:, i * Q : (i + 1) * Q]
    return z * f64(c)

@@ -1,0 +1,55 @@
+import concourse.mybir as mybir
+from concourse.masks import make_identity
+
+BF16, F32, U16 = mybir.dt.bfloat16, mybir.dt.float32, mybir.dt.uint16
+
+P = 128
+SEQS, TOKENS = 2, 256
+K, N = 512, 256
+K_BLOCKS = K // P
+PIECE = N // SEQS
+PIECE_COLS = PIECE // 16
+
+FLOPS = 2 * K * P * N
+
+
+def tile_scatter_matmul_kernel(tc, base, x, w, c, offs, out):
+    nc = tc.nc
+    with (
+        tc.tile_pool(name="held", bufs=1) as held,
+        tc.psum_pool(name="banks", bufs=1) as banks,
+    ):
+        offsets = held.tile([P, N // 16], U16, name="offsets")
+        nc.sync.dma_start(offsets[:], offs)
+        base_sb = held.tile([P, SEQS, TOKENS], BF16, name="base_sb")
+        nc.scalar.dma_start(base_sb[:], base.rearrange("i m t -> m i t"))
+        x_sb = held.tile([P, K_BLOCKS, N], BF16, name="x_sb")
+        nc.sync.dma_start(x_sb[:], x.rearrange("(b p) n -> p b n", p=P))
+        w_sb = held.tile([P, K_BLOCKS, P], BF16, name="w_sb")
+        nc.scalar.dma_start(w_sb[:], w.rearrange("(b p) m -> p b m", p=P))
+        c_all = held.tile([P, TOKENS], F32, name="c_all")
+        nc.gpsimd.dma_start(c_all[:], c.rearrange("o t -> (o t)").partition_broadcast(P))
+
+        ident = held.tile([P, P], BF16, name="ident")
+        make_identity(nc, ident[:])
+
+        windows = [banks.tile([P, TOKENS], F32, name=f"window{i}") for i in range(SEQS)]
+        for i in range(SEQS):
+            nc.tensor.matmul(windows[i][:], ident[:], base_sb[:, i, :], start=True, stop=False)
+
+        for i in range(SEQS):
+            piece = offsets[:, i * PIECE_COLS : (i + 1) * PIECE_COLS]
+            for b in range(K_BLOCKS):
+                nc.tensor.matmul(
+                    windows[i][:].indirect(piece),
+                    w_sb[:, b, :],
+                    x_sb[:, b, i * PIECE : (i + 1) * PIECE],
+                    start=False,
+                    stop=(b == K_BLOCKS - 1),
+                )
+
+        for i in range(SEQS):
+            scaled = held.tile([P, TOKENS], F32, name=f"scaled{i}")
+            nc.vector.tensor_tensor(scaled[:], windows[i][:], c_all[:], mybir.AluOpType.mult)
+            store_queue = nc.sync if i == 0 else nc.scalar
+            store_queue.dma_start(out[i], scaled[:])

@@ -19,6 +19,8 @@ def tile_scatter_matmul_kernel(tc, base, x, w, c, offs, out):
         tc.tile_pool(name="held", bufs=1) as held,
         tc.psum_pool(name="banks", bufs=1) as banks,
     ):
+        c_row = held.tile([1, TOKENS], F32, name="c_row")
+        nc.sync.dma_start(c_row[:], c)
         offsets = held.tile([P, N // 16], U16, name="offsets")
         nc.sync.dma_start(offsets[:], offs)
         base_sb = held.tile([P, SEQS, TOKENS], BF16, name="base_sb")
@@ -27,11 +29,16 @@ def tile_scatter_matmul_kernel(tc, base, x, w, c, offs, out):
         nc.sync.dma_start(x_sb[:], x.rearrange("(b p) n -> p b n", p=P))
         w_sb = held.tile([P, K_BLOCKS, P], BF16, name="w_sb")
         nc.scalar.dma_start(w_sb[:], w.rearrange("(b p) m -> p b m", p=P))
-        c_all = held.tile([P, TOKENS], F32, name="c_all")
-        nc.gpsimd.dma_start(c_all[:], c.rearrange("o t -> (o t)").partition_broadcast(P))
 
         ident = held.tile([P, P], BF16, name="ident")
         make_identity(nc, ident[:])
+
+        ones_row = held.tile([1, P], F32, name="ones_row")
+        nc.vector.memset(ones_row[:], 1.0)
+        c_bank = banks.tile([P, TOKENS], F32, name="c_bank")
+        nc.tensor.matmul(c_bank[:], ones_row[:], c_row[:], start=True, stop=True)
+        c_all = held.tile([P, TOKENS], F32, name="c_all")
+        nc.vector.tensor_copy(c_all[:], c_bank[:])
 
         windows = [banks.tile([P, TOKENS], F32, name=f"window{i}") for i in range(SEQS)]
         for i in range(SEQS):

@@ -25,10 +25,11 @@ def tile_scatter_matmul_kernel(tc, base, x, w, c, offs, out):
         nc.sync.dma_start(offsets[:], offs)
         base_sb = held.tile([P, SEQS, TOKENS], BF16, name="base_sb")
         nc.scalar.dma_start(base_sb[:], base.rearrange("i m t -> m i t"))
-        x_sb = held.tile([P, K_BLOCKS, N], BF16, name="x_sb")
-        nc.sync.dma_start(x_sb[:], x.rearrange("(b p) n -> p b n", p=P))
-        w_sb = held.tile([P, K_BLOCKS, P], BF16, name="w_sb")
-        nc.scalar.dma_start(w_sb[:], w.rearrange("(b p) m -> p b m", p=P))
+        x_blocks = [held.tile([P, N], BF16, name=f"x_block{b}") for b in range(K_BLOCKS)]
+        w_blocks = [held.tile([P, P], BF16, name=f"w_block{b}") for b in range(K_BLOCKS)]
+        for b in range(K_BLOCKS):
+            nc.sync.dma_start(x_blocks[b][:], x[b * P : (b + 1) * P, :])
+            nc.scalar.dma_start(w_blocks[b][:], w[b * P : (b + 1) * P, :])
 
         ident = held.tile([P, P], BF16, name="ident")
         make_identity(nc, ident[:])
@@ -44,13 +45,12 @@ def tile_scatter_matmul_kernel(tc, base, x, w, c, offs, out):
         for i in range(SEQS):
             nc.tensor.matmul(windows[i][:], ident[:], base_sb[:, i, :], start=True, stop=False)
 
-        for i in range(SEQS):
-            piece = offsets[:, i * PIECE_COLS : (i + 1) * PIECE_COLS]
-            for b in range(K_BLOCKS):
+        for b in range(K_BLOCKS):
+            for i in range(SEQS):
                 nc.tensor.matmul(
-                    windows[i][:].indirect(piece),
-                    w_sb[:, b, :],
-                    x_sb[:, b, i * PIECE : (i + 1) * PIECE],
+                    windows[i][:].indirect(offsets[:, i * PIECE_COLS : (i + 1) * PIECE_COLS]),
+                    w_blocks[b][:],
+                    x_blocks[b][:, i * PIECE : (i + 1) * PIECE],
                     start=False,
                     stop=(b == K_BLOCKS - 1),
                 )

@@ -9,6 +9,7 @@ K, N = 512, 256
 K_BLOCKS = K // P
 PIECE = N // SEQS
 PIECE_COLS = PIECE // 16
+WARM_MATMULS = 16
 
 FLOPS = 2 * K * P * N
 
@@ -25,11 +26,16 @@ def tile_scatter_matmul_kernel(tc, base, x, w, c, offs, out):
         nc.sync.dma_start(offsets[:], offs)
         base_sb = held.tile([P, SEQS, TOKENS], BF16, name="base_sb")
         nc.scalar.dma_start(base_sb[:], base.rearrange("i m t -> m i t"))
-        x_blocks = [held.tile([P, N], BF16, name=f"x_block{b}") for b in range(K_BLOCKS)]
-        w_blocks = [held.tile([P, P], BF16, name=f"w_block{b}") for b in range(K_BLOCKS)]
-        for b in range(K_BLOCKS):
-            nc.sync.dma_start(x_blocks[b][:], x[b * P : (b + 1) * P, :])
-            nc.scalar.dma_start(w_blocks[b][:], w[b * P : (b + 1) * P, :])
+        x_sb = held.tile([P, K_BLOCKS, N], BF16, name="x_sb")
+        nc.sync.dma_start(x_sb[:], x.rearrange("(b p) n -> p b n", p=P))
+        w_sb = held.tile([P, K_BLOCKS, P], BF16, name="w_sb")
+        nc.scalar.dma_start(w_sb[:], w.rearrange("(b p) m -> p b m", p=P))
+
+        zeros = held.tile([P, P], BF16, name="zeros")
+        nc.vector.memset(zeros[:], 0.0)
+        warm_bank = banks.tile([P, P], F32, name="warm_bank")
+        for warm in range(WARM_MATMULS):
+            nc.tensor.matmul(warm_bank[:], zeros[:], zeros[:], start=True, stop=True)
 
         ident = held.tile([P, P], BF16, name="ident")
         make_identity(nc, ident[:])
@@ -45,12 +51,13 @@ def tile_scatter_matmul_kernel(tc, base, x, w, c, offs, out):
         for i in range(SEQS):
             nc.tensor.matmul(windows[i][:], ident[:], base_sb[:, i, :], start=True, stop=False)
 
-        for b in range(K_BLOCKS):
-            for i in range(SEQS):
+        for i in range(SEQS):
+            piece = offsets[:, i * PIECE_COLS : (i + 1) * PIECE_COLS]
+            for b in range(K_BLOCKS):
                 nc.tensor.matmul(
-                    windows[i][:].indirect(offsets[:, i * PIECE_COLS : (i + 1) * PIECE_COLS]),
-                    w_blocks[b][:],
-                    x_blocks[b][:, i * PIECE : (i + 1) * PIECE],
+                    windows[i][:].indirect(piece),
+                    w_sb[:, b, :],
+                    x_sb[:, b, i * PIECE : (i + 1) * PIECE],
                     start=False,
                     stop=(b == K_BLOCKS - 1),
                 )

@@ -9,7 +9,7 @@ K, N = 512, 256
 K_BLOCKS = K // P
 PIECE = N // SEQS
 PIECE_COLS = PIECE // 16
-WARM_MATMULS = 16
+WARM_MATMULS = 12
 
 FLOPS = 2 * K * P * N
 

@@ -40,10 +40,13 @@ def tile_scatter_matmul_kernel(tc, base, x, w, c, offs, out):
         ident = held.tile([P, P], BF16, name="ident")
         make_identity(nc, ident[:])
 
-        ones_row = held.tile([1, P], F32, name="ones_row")
-        nc.vector.memset(ones_row[:], 1.0)
+        ones = held.tile([P, P], F32, name="ones")
+        nc.vector.memset(ones[:], 1.0)
+        c_padded = held.tile([P, TOKENS], F32, name="c_padded")
+        nc.vector.memset(c_padded[:], 0.0)
+        nc.vector.tensor_copy(c_padded[0:1, :], c_row[:])
         c_bank = banks.tile([P, TOKENS], F32, name="c_bank")
-        nc.tensor.matmul(c_bank[:], ones_row[:], c_row[:], start=True, stop=True)
+        nc.tensor.matmul(c_bank[:], ones[:], c_padded[:], start=True, stop=True)
         c_all = held.tile([P, TOKENS], F32, name="c_all")
         nc.vector.tensor_copy(c_all[:], c_bank[:])
 

@@ -27,9 +27,9 @@ def tile_scatter_matmul_kernel(tc, base, x, w, c, offs, out):
         base_sb = held.tile([P, SEQS, TOKENS], BF16, name="base_sb")
         nc.scalar.dma_start(base_sb[:], base.rearrange("i m t -> m i t"))
         x_sb = held.tile([P, K_BLOCKS, N], BF16, name="x_sb")
-        nc.sync.dma_start(x_sb[:], x.rearrange("(b p) n -> p b n", p=P))
+        nc.sync.dma_start(x_sb[:], x.rearrange("(p b) n -> p b n", p=P))
         w_sb = held.tile([P, K_BLOCKS, P], BF16, name="w_sb")
-        nc.scalar.dma_start(w_sb[:], w.rearrange("(b p) m -> p b m", p=P))
+        nc.scalar.dma_start(w_sb[:], w.rearrange("(p b) m -> p b m", p=P))
 
         zeros = held.tile([P, P], BF16, name="zeros")
         nc.vector.memset(zeros[:], 0.0)

@@ -38,7 +38,8 @@ def tile_scatter_matmul_kernel(tc, base, x, w, c, offs, out):
             nc.tensor.matmul(warm_bank[:], zeros[:], zeros[:], start=True, stop=True)
 
         ident = held.tile([P, P], BF16, name="ident")
-        make_identity(nc, ident[:])
+        nc.vector.memset(ident[:], 0.0)
+        make_identity(nc, ident[:], nomemset=True)
 
         ones = held.tile([P, P], F32, name="ones")
         nc.vector.memset(ones[:], 1.0)

@@ -20,8 +20,8 @@ def tile_scatter_matmul_kernel(tc, base, x, w, c, offs, out):
         tc.tile_pool(name="held", bufs=1) as held,
         tc.psum_pool(name="banks", bufs=1) as banks,
     ):
-        c_row = held.tile([1, TOKENS], F32, name="c_row")
-        nc.sync.dma_start(c_row[:], c)
+        c_pairs = held.tile([P, TOKENS // P], F32, name="c_pairs")
+        nc.sync.dma_start(c_pairs[:], c.rearrange("o (p j) -> p (o j)", p=P))
         offsets = held.tile([P, N // 16], U16, name="offsets")
         nc.sync.dma_start(offsets[:], offs)
         base_sb = held.tile([P, SEQS, TOKENS], BF16, name="base_sb")
@@ -41,15 +41,19 @@ def tile_scatter_matmul_kernel(tc, base, x, w, c, offs, out):
         nc.vector.memset(ident[:], 0.0)
         make_identity(nc, ident[:], nomemset=True)
 
-        ones = held.tile([P, P], F32, name="ones")
-        nc.vector.memset(ones[:], 1.0)
-        c_padded = held.tile([P, TOKENS], F32, name="c_padded")
-        nc.vector.memset(c_padded[:], 0.0)
-        nc.vector.tensor_copy(c_padded[0:1, :], c_row[:])
+        ident_f32 = held.tile([P, P], F32, name="ident_f32")
+        nc.vector.memset(ident_f32[:], 0.0)
+        make_identity(nc, ident_f32[:], nomemset=True)
         c_bank = banks.tile([P, TOKENS], F32, name="c_bank")
-        nc.tensor.matmul(c_bank[:], ones[:], c_padded[:], start=True, stop=True)
+        for j in range(TOKENS // P):
+            nc.tensor.transpose(
+                c_bank[:, j * P : (j + 1) * P], c_pairs[:, j : j + 1].to_broadcast([P, P]), ident_f32[:]
+            )
         c_all = held.tile([P, TOKENS], F32, name="c_all")
-        nc.vector.tensor_copy(c_all[:], c_bank[:])
+        nc.vector.tensor_copy(
+            c_all[:].rearrange("p (k j) -> p k j", j=TOKENS // P),
+            c_bank[:].rearrange("p (j k) -> p k j", j=TOKENS // P),
+        )
 
         windows = [banks.tile([P, TOKENS], F32, name=f"window{i}") for i in range(SEQS)]
         for i in range(SEQS):

@@ -37,13 +37,16 @@ def tile_scatter_matmul_kernel(tc, base, x, w, c, offs, out):
         for warm in range(WARM_MATMULS):
             nc.tensor.matmul(warm_bank[:], zeros[:], zeros[:], start=True, stop=True)
 
-        ident = held.tile([P, P], BF16, name="ident")
-        nc.vector.memset(ident[:], 0.0)
-        make_identity(nc, ident[:], nomemset=True)
-
         ident_f32 = held.tile([P, P], F32, name="ident_f32")
         nc.vector.memset(ident_f32[:], 0.0)
         make_identity(nc, ident_f32[:], nomemset=True)
+        ident = held.tile([P, P], BF16, name="ident")
+        nc.vector.tensor_copy(ident[:], ident_f32[:])
+
+        windows = [banks.tile([P, TOKENS], F32, name=f"window{i}") for i in range(SEQS)]
+        for i in range(SEQS):
+            nc.tensor.matmul(windows[i][:], ident[:], base_sb[:, i, :], start=True, stop=False)
+
         c_bank = banks.tile([P, TOKENS], F32, name="c_bank")
         for j in range(TOKENS // P):
             nc.tensor.transpose(
@@ -54,10 +57,6 @@ def tile_scatter_matmul_kernel(tc, base, x, w, c, offs, out):
             c_all[:].rearrange("p (k j) -> p k j", j=TOKENS // P),
             c_bank[:].rearrange("p (j k) -> p k j", j=TOKENS // P),
         )
-
-        windows = [banks.tile([P, TOKENS], F32, name=f"window{i}") for i in range(SEQS)]
-        for i in range(SEQS):
-            nc.tensor.matmul(windows[i][:], ident[:], base_sb[:, i, :], start=True, stop=False)
 
         for i in range(SEQS):
             piece = offsets[:, i * PIECE_COLS : (i + 1) * PIECE_COLS]

@@ -9,6 +9,8 @@ K, N = 512, 256
 K_BLOCKS = K // P
 PIECE = N // SEQS
 PIECE_COLS = PIECE // 16
+X_PARTS = 2
+PART_BLOCKS = K_BLOCKS // X_PARTS
 WARM_MATMULS = 12
 
 FLOPS = 2 * K * P * N
@@ -26,10 +28,12 @@ def tile_scatter_matmul_kernel(tc, base, x, w, c, offs, out):
         nc.sync.dma_start(offsets[:], offs)
         base_sb = held.tile([P, SEQS, TOKENS], BF16, name="base_sb")
         nc.scalar.dma_start(base_sb[:], base.rearrange("i m t -> m i t"))
-        x_sb = held.tile([P, K_BLOCKS, N], BF16, name="x_sb")
-        nc.sync.dma_start(x_sb[:], x.rearrange("(p b) n -> p b n", p=P))
+        x_blocks = x.rearrange("(p b) n -> p b n", p=P)
+        x_parts = [held.tile([P, PART_BLOCKS, N], BF16, name=f"x_part{h}") for h in range(X_PARTS)]
+        nc.sync.dma_start(x_parts[0][:], x_blocks[:, 0:PART_BLOCKS, :])
         w_sb = held.tile([P, K_BLOCKS, P], BF16, name="w_sb")
         nc.scalar.dma_start(w_sb[:], w.rearrange("(p b) m -> p b m", p=P))
+        nc.scalar.dma_start(x_parts[1][:], x_blocks[:, PART_BLOCKS:K_BLOCKS, :])
 
         zeros = held.tile([P, P], BF16, name="zeros")
         nc.vector.memset(zeros[:], 0.0)
@@ -58,16 +62,18 @@ def tile_scatter_matmul_kernel(tc, base, x, w, c, offs, out):
             c_bank[:].rearrange("p (j k) -> p k j", j=TOKENS // P),
         )
 
-        for i in range(SEQS):
-            piece = offsets[:, i * PIECE_COLS : (i + 1) * PIECE_COLS]
-            for b in range(K_BLOCKS):
-                nc.tensor.matmul(
-                    windows[i][:].indirect(piece),
-                    w_sb[:, b, :],
-                    x_sb[:, b, i * PIECE : (i + 1) * PIECE],
-                    start=False,
-                    stop=(b == K_BLOCKS - 1),
-                )
+        for h in range(X_PARTS):
+            for i in range(SEQS):
+                piece = offsets[:, i * PIECE_COLS : (i + 1) * PIECE_COLS]
+                for r in range(PART_BLOCKS):
+                    b = h * PART_BLOCKS + r
+                    nc.tensor.matmul(
+                        windows[i][:].indirect(piece),
+                        w_sb[:, b, :],
+                        x_parts[h][:, r, i * PIECE : (i + 1) * PIECE],
+                        start=False,
+                        stop=(b == K_BLOCKS - 1),
+                    )
 
         for i in range(SEQS):
             scaled = held.tile([P, TOKENS], F32, name=f"scaled{i}")

@@ -11,7 +11,7 @@ PIECE = N // SEQS
 PIECE_COLS = PIECE // 16
 X_PARTS = 2
 PART_BLOCKS = K_BLOCKS // X_PARTS
-WARM_MATMULS = 12
+WARM_MATMULS = 10
 
 FLOPS = 2 * K * P * N
 

@@ -62,18 +62,16 @@ def tile_scatter_matmul_kernel(tc, base, x, w, c, offs, out):
             c_bank[:].rearrange("p (j k) -> p k j", j=TOKENS // P),
         )
 
-        for h in range(X_PARTS):
-            for i in range(SEQS):
-                piece = offsets[:, i * PIECE_COLS : (i + 1) * PIECE_COLS]
-                for r in range(PART_BLOCKS):
-                    b = h * PART_BLOCKS + r
-                    nc.tensor.matmul(
-                        windows[i][:].indirect(piece),
-                        w_sb[:, b, :],
-                        x_parts[h][:, r, i * PIECE : (i + 1) * PIECE],
-                        start=False,
-                        stop=(b == K_BLOCKS - 1),
-                    )
+        for i in range(SEQS):
+            piece = offsets[:, i * PIECE_COLS : (i + 1) * PIECE_COLS]
+            for b in range(K_BLOCKS):
+                nc.tensor.matmul(
+                    windows[i][:].indirect(piece),
+                    w_sb[:, b, :],
+                    x_parts[b // PART_BLOCKS][:, b % PART_BLOCKS, i * PIECE : (i + 1) * PIECE],
+                    start=False,
+                    stop=(b == K_BLOCKS - 1),
+                )
 
         for i in range(SEQS):
             scaled = held.tile([P, TOKENS], F32, name=f"scaled{i}")

@@ -62,16 +62,16 @@ def tile_scatter_matmul_kernel(tc, base, x, w, c, offs, out):
             c_bank[:].rearrange("p (j k) -> p k j", j=TOKENS // P),
         )
 
-        for i in range(SEQS):
-            piece = offsets[:, i * PIECE_COLS : (i + 1) * PIECE_COLS]
-            for b in range(K_BLOCKS):
-                nc.tensor.matmul(
-                    windows[i][:].indirect(piece),
-                    w_sb[:, b, :],
-                    x_parts[b // PART_BLOCKS][:, b % PART_BLOCKS, i * PIECE : (i + 1) * PIECE],
-                    start=False,
-                    stop=(b == K_BLOCKS - 1),
-                )
+        run = [(0, b) for b in range(PART_BLOCKS)] + [(1, 0)] + [(0, b) for b in range(PART_BLOCKS, K_BLOCKS)]
+        run += [(1, b) for b in range(1, K_BLOCKS)]
+        for i, b in run:
+            nc.tensor.matmul(
+                windows[i][:].indirect(offsets[:, i * PIECE_COLS : (i + 1) * PIECE_COLS]),
+                w_sb[:, b, :],
+                x_parts[b // PART_BLOCKS][:, b % PART_BLOCKS, i * PIECE : (i + 1) * PIECE],
+                start=False,
+                stop=(b == K_BLOCKS - 1),
+            )
 
         for i in range(SEQS):
             scaled = held.tile([P, TOKENS], F32, name=f"scaled{i}")

@@ -30,9 +30,9 @@ def tile_scatter_matmul_kernel(tc, base, x, w, c, offs, out):
         nc.scalar.dma_start(base_sb[:], base.rearrange("i m t -> m i t"))
         x_blocks = x.rearrange("(p b) n -> p b n", p=P)
         x_parts = [held.tile([P, PART_BLOCKS, N], BF16, name=f"x_part{h}") for h in range(X_PARTS)]
-        nc.sync.dma_start(x_parts[0][:], x_blocks[:, 0:PART_BLOCKS, :])
         w_sb = held.tile([P, K_BLOCKS, P], BF16, name="w_sb")
         nc.scalar.dma_start(w_sb[:], w.rearrange("(p b) m -> p b m", p=P))
+        nc.scalar.dma_start(x_parts[0][:], x_blocks[:, 0:PART_BLOCKS, :])
         nc.scalar.dma_start(x_parts[1][:], x_blocks[:, PART_BLOCKS:K_BLOCKS, :])
 
         zeros = held.tile([P, P], BF16, name="zeros")
@@ -76,5 +76,4 @@ def tile_scatter_matmul_kernel(tc, base, x, w, c, offs, out):
         for i in range(SEQS):
             scaled = held.tile([P, TOKENS], F32, name=f"scaled{i}")
             nc.vector.tensor_tensor(scaled[:], windows[i][:], c_all[:], mybir.AluOpType.mult)
-            store_queue = nc.sync if i == 0 else nc.scalar
-            store_queue.dma_start(out[i], scaled[:])
+            nc.sync.dma_start(out[i], scaled[:])

@@ -9,8 +9,7 @@ K, N = 512, 256
 K_BLOCKS = K // P
 PIECE = N // SEQS
 PIECE_COLS = PIECE // 16
-X_PARTS = 2
-PART_BLOCKS = K_BLOCKS // X_PARTS
+FIRST_BLOCKS = 1
 WARM_MATMULS = 10
 
 FLOPS = 2 * K * P * N
@@ -29,11 +28,13 @@ def tile_scatter_matmul_kernel(tc, base, x, w, c, offs, out):
         base_sb = held.tile([P, SEQS, TOKENS], BF16, name="base_sb")
         nc.scalar.dma_start(base_sb[:], base.rearrange("i m t -> m i t"))
         x_blocks = x.rearrange("(p b) n -> p b n", p=P)
-        x_parts = [held.tile([P, PART_BLOCKS, N], BF16, name=f"x_part{h}") for h in range(X_PARTS)]
+        x_first = held.tile([P, FIRST_BLOCKS, N], BF16, name="x_first")
+        x_rest = held.tile([P, K_BLOCKS - FIRST_BLOCKS, N], BF16, name="x_rest")
         w_sb = held.tile([P, K_BLOCKS, P], BF16, name="w_sb")
         nc.scalar.dma_start(w_sb[:], w.rearrange("(p b) m -> p b m", p=P))
-        nc.scalar.dma_start(x_parts[0][:], x_blocks[:, 0:PART_BLOCKS, :])
-        nc.scalar.dma_start(x_parts[1][:], x_blocks[:, PART_BLOCKS:K_BLOCKS, :])
+        nc.scalar.dma_start(x_first[:], x_blocks[:, 0:FIRST_BLOCKS, :])
+        nc.scalar.dma_start(x_rest[:], x_blocks[:, FIRST_BLOCKS:K_BLOCKS, :])
+        x_home = [(x_first, b) for b in range(FIRST_BLOCKS)] + [(x_rest, b) for b in range(K_BLOCKS - FIRST_BLOCKS)]
 
         zeros = held.tile([P, P], BF16, name="zeros")
         nc.vector.memset(zeros[:], 0.0)
@@ -62,13 +63,14 @@ def tile_scatter_matmul_kernel(tc, base, x, w, c, offs, out):
             c_bank[:].rearrange("p (j k) -> p k j", j=TOKENS // P),
         )
 
-        run = [(0, b) for b in range(PART_BLOCKS)] + [(1, 0)] + [(0, b) for b in range(PART_BLOCKS, K_BLOCKS)]
-        run += [(1, b) for b in range(1, K_BLOCKS)]
+        run = [(i, b) for i in range(SEQS) for b in range(FIRST_BLOCKS)]
+        run += [(i, b) for i in range(SEQS) for b in range(FIRST_BLOCKS, K_BLOCKS)]
         for i, b in run:
+            x_tile, x_place = x_home[b]
             nc.tensor.matmul(
                 windows[i][:].indirect(offsets[:, i * PIECE_COLS : (i + 1) * PIECE_COLS]),
                 w_sb[:, b, :],
-                x_parts[b // PART_BLOCKS][:, b % PART_BLOCKS, i * PIECE : (i + 1) * PIECE],
+                x_tile[:, x_place, i * PIECE : (i + 1) * PIECE],
                 start=False,
                 stop=(b == K_BLOCKS - 1),
             )

@@ -9,7 +9,8 @@ K, N = 512, 256
 K_BLOCKS = K // P
 PIECE = N // SEQS
 PIECE_COLS = PIECE // 16
-FIRST_BLOCKS = 1
+UNITS = K_BLOCKS * SEQS
+FIRST_UNITS = 3
 WARM_MATMULS = 10
 
 FLOPS = 2 * K * P * N
@@ -27,14 +28,14 @@ def tile_scatter_matmul_kernel(tc, base, x, w, c, offs, out):
         nc.sync.dma_start(offsets[:], offs)
         base_sb = held.tile([P, SEQS, TOKENS], BF16, name="base_sb")
         nc.scalar.dma_start(base_sb[:], base.rearrange("i m t -> m i t"))
-        x_blocks = x.rearrange("(p b) n -> p b n", p=P)
-        x_first = held.tile([P, FIRST_BLOCKS, N], BF16, name="x_first")
-        x_rest = held.tile([P, K_BLOCKS - FIRST_BLOCKS, N], BF16, name="x_rest")
+        x_units = x.rearrange("(p b) (i j) -> p (b i) j", p=P, i=SEQS)
+        x_first = held.tile([P, FIRST_UNITS, PIECE], BF16, name="x_first")
+        x_rest = held.tile([P, UNITS - FIRST_UNITS, PIECE], BF16, name="x_rest")
         w_sb = held.tile([P, K_BLOCKS, P], BF16, name="w_sb")
         nc.scalar.dma_start(w_sb[:], w.rearrange("(p b) m -> p b m", p=P))
-        nc.scalar.dma_start(x_first[:], x_blocks[:, 0:FIRST_BLOCKS, :])
-        nc.scalar.dma_start(x_rest[:], x_blocks[:, FIRST_BLOCKS:K_BLOCKS, :])
-        x_home = [(x_first, b) for b in range(FIRST_BLOCKS)] + [(x_rest, b) for b in range(K_BLOCKS - FIRST_BLOCKS)]
+        nc.scalar.dma_start(x_first[:], x_units[:, 0:FIRST_UNITS, :])
+        nc.scalar.dma_start(x_rest[:], x_units[:, FIRST_UNITS:UNITS, :])
+        x_home = [(x_first, u) for u in range(FIRST_UNITS)] + [(x_rest, u) for u in range(UNITS - FIRST_UNITS)]
 
         zeros = held.tile([P, P], BF16, name="zeros")
         nc.vector.memset(zeros[:], 0.0)
@@ -63,14 +64,14 @@ def tile_scatter_matmul_kernel(tc, base, x, w, c, offs, out):
             c_bank[:].rearrange("p (j k) -> p k j", j=TOKENS // P),
         )
 
-        run = [(i, b) for i in range(SEQS) for b in range(FIRST_BLOCKS)]
-        run += [(i, b) for i in range(SEQS) for b in range(FIRST_BLOCKS, K_BLOCKS)]
+        run = [(i, b) for b in range(K_BLOCKS) for i in range(SEQS) if b * SEQS + i < FIRST_UNITS]
+        run += [(i, b) for i in range(SEQS) for b in range(K_BLOCKS) if b * SEQS + i >= FIRST_UNITS]
         for i, b in run:
-            x_tile, x_place = x_home[b]
+            x_tile, x_place = x_home[b * SEQS + i]
             nc.tensor.matmul(
                 windows[i][:].indirect(offsets[:, i * PIECE_COLS : (i + 1) * PIECE_COLS]),
                 w_sb[:, b, :],
-                x_tile[:, x_place, i * PIECE : (i + 1) * PIECE],
+                x_tile[:, x_place, :],
                 start=False,
                 stop=(b == K_BLOCKS - 1),
             )

@@ -37,11 +37,12 @@ def tile_scatter_matmul_kernel(tc, base, x, w, c, offs, out):
         nc.scalar.dma_start(x_rest[:], x_units[:, FIRST_UNITS:UNITS, :])
         x_home = [(x_first, u) for u in range(FIRST_UNITS)] + [(x_rest, u) for u in range(UNITS - FIRST_UNITS)]
 
-        zeros = held.tile([P, P], BF16, name="zeros")
-        nc.vector.memset(zeros[:], 0.0)
+        zero_column = held.tile([P, 1], BF16, name="zero_column")
+        nc.vector.memset(zero_column[:], 0.0)
+        zeros = zero_column[:, 0:1].to_broadcast([P, P])
         warm_bank = banks.tile([P, P], F32, name="warm_bank")
         for warm in range(WARM_MATMULS):
-            nc.tensor.matmul(warm_bank[:], zeros[:], zeros[:], start=True, stop=True)
+            nc.tensor.matmul(warm_bank[:], zeros, zeros, start=True, stop=True)
 
         ident_f32 = held.tile([P, P], F32, name="ident_f32")
         nc.vector.memset(ident_f32[:], 0.0)

@@ -11,7 +11,8 @@ PIECE = N // SEQS
 PIECE_COLS = PIECE // 16
 UNITS = K_BLOCKS * SEQS
 FIRST_UNITS = 3
-WARM_MATMULS = 10
+WARM_MATMULS = 2
+WARM_COLUMNS = 512
 
 FLOPS = 2 * K * P * N
 
@@ -39,10 +40,11 @@ def tile_scatter_matmul_kernel(tc, base, x, w, c, offs, out):
 
         zero_column = held.tile([P, 1], BF16, name="zero_column")
         nc.vector.memset(zero_column[:], 0.0)
-        zeros = zero_column[:, 0:1].to_broadcast([P, P])
-        warm_bank = banks.tile([P, P], F32, name="warm_bank")
+        zero_weights = zero_column[:, 0:1].to_broadcast([P, P])
+        zero_stream = zero_column[:, 0:1].to_broadcast([P, WARM_COLUMNS])
+        warm_bank = banks.tile([P, WARM_COLUMNS], F32, name="warm_bank")
         for warm in range(WARM_MATMULS):
-            nc.tensor.matmul(warm_bank[:], zeros, zeros, start=True, stop=True)
+            nc.tensor.matmul(warm_bank[:], zero_weights, zero_stream, start=True, stop=True)
 
         ident_f32 = held.tile([P, P], F32, name="ident_f32")
         nc.vector.memset(ident_f32[:], 0.0)

@@ -11,7 +11,7 @@ PIECE = N // SEQS
 PIECE_COLS = PIECE // 16
 UNITS = K_BLOCKS * SEQS
 FIRST_UNITS = 3
-WARM_MATMULS = 2
+WARM_MATMULS = 3
 WARM_COLUMNS = 512
 
 FLOPS = 2 * K * P * N

@@ -11,6 +11,7 @@ PIECE = N // SEQS
 PIECE_COLS = PIECE // 16
 UNITS = K_BLOCKS * SEQS
 FIRST_UNITS = 3
+DMA_ALIGN = 256
 WARM_MATMULS = 3
 WARM_COLUMNS = 512
 
@@ -27,12 +28,12 @@ def tile_scatter_matmul_kernel(tc, base, x, w, c, offs, out):
         nc.sync.dma_start(c_pairs[:], c.rearrange("o (p j) -> p (o j)", p=P))
         offsets = held.tile([P, N // 16], U16, name="offsets")
         nc.sync.dma_start(offsets[:], offs)
-        base_sb = held.tile([P, SEQS, TOKENS], BF16, name="base_sb")
+        base_sb = held.tile([P, SEQS, TOKENS], BF16, name="base_sb", align_bytes=DMA_ALIGN)
         nc.scalar.dma_start(base_sb[:], base.rearrange("i m t -> m i t"))
         x_units = x.rearrange("(p b) (i j) -> p (b i) j", p=P, i=SEQS)
-        x_first = held.tile([P, FIRST_UNITS, PIECE], BF16, name="x_first")
-        x_rest = held.tile([P, UNITS - FIRST_UNITS, PIECE], BF16, name="x_rest")
-        w_sb = held.tile([P, K_BLOCKS, P], BF16, name="w_sb")
+        x_first = held.tile([P, FIRST_UNITS, PIECE], BF16, name="x_first", align_bytes=DMA_ALIGN)
+        x_rest = held.tile([P, UNITS - FIRST_UNITS, PIECE], BF16, name="x_rest", align_bytes=DMA_ALIGN)
+        w_sb = held.tile([P, K_BLOCKS, P], BF16, name="w_sb", align_bytes=DMA_ALIGN)
         nc.scalar.dma_start(w_sb[:], w.rearrange("(p b) m -> p b m", p=P))
         nc.scalar.dma_start(x_first[:], x_units[:, 0:FIRST_UNITS, :])
         nc.scalar.dma_start(x_rest[:], x_units[:, FIRST_UNITS:UNITS, :])
@@ -80,6 +81,6 @@ def tile_scatter_matmul_kernel(tc, base, x, w, c, offs, out):
             )
 
         for i in range(SEQS):
-            scaled = held.tile([P, TOKENS], F32, name=f"scaled{i}")
+            scaled = held.tile([P, TOKENS], F32, name=f"scaled{i}", align_bytes=DMA_ALIGN)
             nc.vector.tensor_tensor(scaled[:], windows[i][:], c_all[:], mybir.AluOpType.mult)
             nc.sync.dma_start(out[i], scaled[:])

@@ -24,7 +24,7 @@ def tile_scatter_matmul_kernel(tc, base, x, w, c, offs, out):
         tc.tile_pool(name="held", bufs=1) as held,
         tc.psum_pool(name="banks", bufs=1) as banks,
     ):
-        c_pairs = held.tile([P, TOKENS // P], F32, name="c_pairs")
+        c_pairs = held.tile([P, TOKENS // P], F32, name="c_pairs", align_bytes=DMA_ALIGN)
         nc.sync.dma_start(c_pairs[:], c.rearrange("o (p j) -> p (o j)", p=P))
         offsets = held.tile([P, N // 16], U16, name="offsets")
         nc.sync.dma_start(offsets[:], offs)
@@ -39,7 +39,7 @@ def tile_scatter_matmul_kernel(tc, base, x, w, c, offs, out):
         nc.scalar.dma_start(x_rest[:], x_units[:, FIRST_UNITS:UNITS, :])
         x_home = [(x_first, u) for u in range(FIRST_UNITS)] + [(x_rest, u) for u in range(UNITS - FIRST_UNITS)]
 
-        zero_column = held.tile([P, 1], BF16, name="zero_column")
+        zero_column = held.tile([P, 1], BF16, name="zero_column", align_bytes=DMA_ALIGN)
         nc.vector.memset(zero_column[:], 0.0)
         zero_weights = zero_column[:, 0:1].to_broadcast([P, P])
         zero_stream = zero_column[:, 0:1].to_broadcast([P, WARM_COLUMNS])
@@ -47,10 +47,10 @@ def tile_scatter_matmul_kernel(tc, base, x, w, c, offs, out):
         for warm in range(WARM_MATMULS):
             nc.tensor.matmul(warm_bank[:], zero_weights, zero_stream, start=True, stop=True)
 
-        ident_f32 = held.tile([P, P], F32, name="ident_f32")
+        ident_f32 = held.tile([P, P], F32, name="ident_f32", align_bytes=DMA_ALIGN)
         nc.vector.memset(ident_f32[:], 0.0)
         make_identity(nc, ident_f32[:], nomemset=True)
-        ident = held.tile([P, P], BF16, name="ident")
+        ident = held.tile([P, P], BF16, name="ident", align_bytes=DMA_ALIGN)
         nc.vector.tensor_copy(ident[:], ident_f32[:])
 
         windows = [banks.tile([P, TOKENS], F32, name=f"window{i}") for i in range(SEQS)]
@@ -62,7 +62,7 @@ def tile_scatter_matmul_kernel(tc, base, x, w, c, offs, out):
             nc.tensor.transpose(
                 c_bank[:, j * P : (j + 1) * P], c_pairs[:, j : j + 1].to_broadcast([P, P]), ident_f32[:]
             )
-        c_all = held.tile([P, TOKENS], F32, name="c_all")
+        c_all = held.tile([P, TOKENS], F32, name="c_all", align_bytes=DMA_ALIGN)
         nc.vector.tensor_copy(
             c_all[:].rearrange("p (k j) -> p k j", j=TOKENS // P),
             c_bank[:].rearrange("p (j k) -> p k j", j=TOKENS // P),

import concourse.mybir as mybir
from concourse.masks import make_identity

BF16, F32, U16 = mybir.dt.bfloat16, mybir.dt.float32, mybir.dt.uint16

P = 128
SEQS, TOKENS = 2, 256
K, N = 512, 256
K_BLOCKS = K // P
PIECE = N // SEQS
PIECE_COLS = PIECE // 16
UNITS = K_BLOCKS * SEQS
FIRST_UNITS = 3
DMA_ALIGN = 256
WARM_MATMULS = 3
WARM_COLUMNS = 512

FLOPS = 2 * K * P * N


def tile_scatter_matmul_kernel(tc, base, x, w, c, offs, out):
    nc = tc.nc
    with (
        tc.tile_pool(name="held", bufs=1) as held,
        tc.psum_pool(name="banks", bufs=1) as banks,
    ):
        c_pairs = held.tile([P, TOKENS // P], F32, name="c_pairs", align_bytes=DMA_ALIGN)
        nc.sync.dma_start(c_pairs[:], c.rearrange("o (p j) -> p (o j)", p=P))
        offsets = held.tile([P, N // 16], U16, name="offsets")
        nc.sync.dma_start(offsets[:], offs)
        base_sb = held.tile([P, SEQS, TOKENS], BF16, name="base_sb", align_bytes=DMA_ALIGN)
        nc.scalar.dma_start(base_sb[:], base.rearrange("i m t -> m i t"))
        x_units = x.rearrange("(p b) (i j) -> p (b i) j", p=P, i=SEQS)
        x_first = held.tile([P, FIRST_UNITS, PIECE], BF16, name="x_first", align_bytes=DMA_ALIGN)
        x_rest = held.tile([P, UNITS - FIRST_UNITS, PIECE], BF16, name="x_rest", align_bytes=DMA_ALIGN)
        w_sb = held.tile([P, K_BLOCKS, P], BF16, name="w_sb", align_bytes=DMA_ALIGN)
        nc.scalar.dma_start(w_sb[:], w.rearrange("(p b) m -> p b m", p=P))
        nc.scalar.dma_start(x_first[:], x_units[:, 0:FIRST_UNITS, :])
        nc.scalar.dma_start(x_rest[:], x_units[:, FIRST_UNITS:UNITS, :])
        x_home = [(x_first, u) for u in range(FIRST_UNITS)] + [(x_rest, u) for u in range(UNITS - FIRST_UNITS)]

        zero_column = held.tile([P, 1], BF16, name="zero_column", align_bytes=DMA_ALIGN)
        nc.vector.memset(zero_column[:], 0.0)
        zero_weights = zero_column[:, 0:1].to_broadcast([P, P])
        zero_stream = zero_column[:, 0:1].to_broadcast([P, WARM_COLUMNS])
        warm_bank = banks.tile([P, WARM_COLUMNS], F32, name="warm_bank")
        for warm in range(WARM_MATMULS):
            nc.tensor.matmul(warm_bank[:], zero_weights, zero_stream, start=True, stop=True)

        ident_f32 = held.tile([P, P], F32, name="ident_f32", align_bytes=DMA_ALIGN)
        nc.vector.memset(ident_f32[:], 0.0)
        make_identity(nc, ident_f32[:], nomemset=True)
        ident = held.tile([P, P], BF16, name="ident", align_bytes=DMA_ALIGN)
        nc.vector.tensor_copy(ident[:], ident_f32[:])

        windows = [banks.tile([P, TOKENS], F32, name=f"window{i}") for i in range(SEQS)]
        for i in range(SEQS):
            nc.tensor.matmul(windows[i][:], ident[:], base_sb[:, i, :], start=True, stop=False)

        c_bank = banks.tile([P, TOKENS], F32, name="c_bank")
        for j in range(TOKENS // P):
            nc.tensor.transpose(
                c_bank[:, j * P : (j + 1) * P], c_pairs[:, j : j + 1].to_broadcast([P, P]), ident_f32[:]
            )
        c_all = held.tile([P, TOKENS], F32, name="c_all", align_bytes=DMA_ALIGN)
        nc.vector.tensor_copy(
            c_all[:].rearrange("p (k j) -> p k j", j=TOKENS // P),
            c_bank[:].rearrange("p (j k) -> p k j", j=TOKENS // P),
        )

        run = [(i, b) for b in range(K_BLOCKS) for i in range(SEQS) if b * SEQS + i < FIRST_UNITS]
        run += [(i, b) for i in range(SEQS) for b in range(K_BLOCKS) if b * SEQS + i >= FIRST_UNITS]
        for i, b in run:
            x_tile, x_place = x_home[b * SEQS + i]
            nc.tensor.matmul(
                windows[i][:].indirect(offsets[:, i * PIECE_COLS : (i + 1) * PIECE_COLS]),
                w_sb[:, b, :],
                x_tile[:, x_place, :],
                start=False,
                stop=(b == K_BLOCKS - 1),
            )

        for i in range(SEQS):
            scaled = held.tile([P, TOKENS], F32, name=f"scaled{i}", align_bytes=DMA_ALIGN)
            nc.vector.tensor_tensor(scaled[:], windows[i][:], c_all[:], mybir.AluOpType.mult)
            nc.sync.dma_start(out[i], scaled[:])
